import numpy as np
import ml_dtypes


def mxq(x, axis, fmt="e4m3"):
    dtype, down = {"e4m3": (ml_dtypes.float8_e4m3fn, 7), "e5m2": (ml_dtypes.float8_e5m2, 14)}[fmt]
    v = np.moveaxis(np.asarray(x, np.float32).astype(ml_dtypes.bfloat16).astype(np.float64), axis, -1)
    blocks = v.reshape(v.shape[:-1] + (-1, 32))
    amax = np.abs(blocks).max(-1, keepdims=True)
    byte = np.maximum(np.where(amax > 0, np.frexp(amax)[1] - 1 + 127, 0) - down, 1)
    scale = np.exp2(byte - 127.0)
    codes = (blocks / scale).astype(np.float32).astype(dtype).astype(np.float64)
    return np.moveaxis((codes * scale).reshape(v.shape), -1, axis)


WIDE = False


def mx_kscale(k):
    if not WIDE:
        return np.ones(k)
    levels = np.array([10, -10, 5, -5, 0])
    if k % 512:
        return np.exp2(np.random.permutation(np.resize(levels, k // 32))).repeat(32)
    a = np.empty((k // 512, 16))
    for p in range(k // 512):
        a[p, :8] = np.random.permutation(np.resize(levels, 8))
        for g in range(8):
            far = levels[np.abs(levels - a[p, g]) >= 10]
            a[p, g + 8] = far[np.random.randint(len(far))]
    return np.exp2(a.ravel()).repeat(32)


BF16 = ml_dtypes.bfloat16


def bf(x):
    return np.asarray(x, np.float32).astype(BF16)


def f64(x):
    return np.asarray(x).astype(np.float64)

def planes(Y):
    n, m = Y.shape
    b = f64(bf(Y)).reshape(n // 32, 32, m)
    amax = np.abs(b).max(1)
    byte = np.clip(np.where(amax > 0, np.frexp(amax)[1] - 1 + 127 - 7, 1), 1, 254)
    codes = (b * np.exp2(127.0 - byte)[:, None, :]).reshape(n, m).astype(np.float32).astype(ml_dtypes.float8_e4m3fn).view(np.uint8)
    words = codes.reshape(n // 512, 128, 4, m).transpose(0, 1, 3, 2)
    return np.ascontiguousarray(words), np.ascontiguousarray(byte.astype(np.uint8).reshape(n // 512, 16, m))


U, G, S, C = 1536, 1024, 2048, 512

def setup_inputs():
    s = mx_kscale(U)
    t = mx_kscale(G)
    cell_rate = 4.0 * np.exp(0.4 * np.random.randn(G, 1))
    n = np.random.poisson(cell_rate * np.random.exponential(1.0, (G, U))).astype(np.float64)
    total = n.sum(axis=1) / 1000.0
    x = 1.5 * np.random.randn(U, S) / np.sqrt(U)
    c = np.random.randn(C, G)
    c = (c - c.mean(axis=1, keepdims=True)) / np.sqrt(G)
    return {
        "counts": bf(n * s[None, :]),
        "outcomes": bf(x / s[:, None]),
        "totals": bf(total / t),
        "contrasts": bf(c / t[None, :]),
        "study_weights": bf(np.exp(0.8 * np.random.randn(S))),
    }

def reference(counts, outcomes, totals, contrasts, study_weights):
    n, x, total = f64(counts), f64(outcomes), f64(totals)
    c, w = f64(contrasts), f64(study_weights)
    sums = mxq(n, 1, "e4m3") @ mxq(x, 0, "e4m3")
    means = sums / total[:, None]
    diff = mxq(c, 1, "e4m3") @ mxq(means, 0, "e4m3")
    y = diff * diff * w[None, :]
    Y = y.T
    words, scales = planes(Y)
    return y, words, scales

@@ -1,0 +1,351 @@
+from contextlib import ExitStack
+
+import concourse.mybir as mybir
+from concourse.masks import make_identity
+
+U, G, S, C = 1536, 1024, 2048, 512
+FLOPS = 2 * G * U * S + 2 * C * G * S
+
+F32 = mybir.dt.float32
+BF16 = mybir.dt.bfloat16
+U32 = mybir.dt.uint32
+I32 = mybir.dt.int32
+U8 = mybir.dt.uint8
+FP8X4 = mybir.dt.float8_e4m3fn_x4
+ACT = mybir.ActivationFunctionType
+
+P = 128
+PACK = 4
+W = 512
+BANKS = 8
+
+
+def tile_resampled_contrast_squares_h3_kernel(tc, counts, outcomes, totals, contrasts, study_weights, out_0, out_1, out_2):
+    nc = tc.nc
+    with ExitStack() as ctx:
+        keep = ctx.enter_context(tc.tile_pool(name="keep", bufs=1))
+        work = ctx.enter_context(tc.tile_pool(name="work", bufs=1))
+        psum = ctx.enter_context(tc.psum_pool(name="psum", bufs=1))
+        ctx.enter_context(tc.manual_schedule())
+
+        tiles = {}
+        idle = list(range(BANKS))
+        bank_of = {}
+
+        def new_bank(key):
+            bank_of[key] = idle[0]
+            idle.remove(bank_of[key])
+            tag = "bank%d" % bank_of[key]
+            tiles[key] = psum.tile([P, W], F32, name=tag, tag=tag)
+            return tiles[key]
+
+        def emptied(key):
+            idle.append(bank_of[key])
+
+        def copy(eng, out, in_):
+            if eng == "S":
+                nc.scalar.copy(out=out, in_=in_)
+            else:
+                nc.vector.tensor_copy(out=out, in_=in_)
+
+        ident = keep.tile([P, P], F32)
+        make_identity(nc, ident[:])
+        tot_raw = keep.tile([P, 2, 16], BF16)
+        w_raw = keep.tile([P, 4, 16], BF16)
+        inv_total = keep.tile([P, 2, PACK], F32)
+        root_w = keep.tile([P, 4, PACK], F32)
+        y_codes = keep.tile([P, 4, W], U32, align_bytes=64)
+        y_scales = keep.tile([P, 4, W], U8, align_bytes=64)
+
+        def load_small():
+            nc.scalar.dma_start(out=w_raw[:, :, 0:PACK], in_=study_weights.rearrange("(g p t) -> p g t", p=P, t=PACK))
+            nc.scalar.dma_start(out=tot_raw[:, :, 0:PACK], in_=totals.rearrange("(h p t) -> p h t", p=P, t=PACK))
+            nc.scalar.activation(out=root_w[:], in_=w_raw[:, :, 0:PACK], func=ACT.Sqrt)
+            nc.vector.reciprocal(out=inv_total[:], in_=tot_raw[:, :, 0:PACK])
+
+        def raw_tile(key):
+            tiles[key] = work.tile([P, PACK, W], BF16, name="raw", tag="raw", bufs=12, align_bytes=64)
+            return tiles[key]
+
+        def woven_tile(key):
+            tiles[key] = work.tile([P, W * PACK], BF16, name="woven", tag="woven", bufs=8, align_bytes=64)
+            return tiles[key]
+
+        def load_rows(which, h, a):
+            raw = raw_tile(("raw", which, h, a))
+            if which == "n":
+                src = counts[h * W:(h + 1) * W, a * W:(a + 1) * W].rearrange("(m t) k -> m t k", t=PACK)
+            else:
+                src = contrasts[:, a * W:(a + 1) * W].rearrange("(t m) k -> m t k", t=PACK)
+            nc.sync.dma_start(out=raw[:], in_=src)
+
+        def load_x(g, a):
+            raw = raw_tile(("raw", "x", g, a))
+            src = outcomes[a * W:(a + 1) * W, g * W:(g + 1) * W].rearrange("(p j) s -> p j s", j=PACK)
+            nc.sync.dma_start(out=raw[:], in_=src)
+
+        def turn_pe(which, h, a):
+            words = tiles["raw", which, h, a][:].rearrange("m t k -> m (t k)").bitcast(F32)
+            for b in range(2):
+                bank = new_bank(("T", which, h, a, b))
+                for i in range(4):
+                    t, u = 2 * b + i // 2, i % 2
+                    nc.tensor.transpose(bank[:, i * P:(i + 1) * P], words[:, 256 * t + u:256 * (t + 1):2], ident[:])
+
+        def turn_out(which, h, a, b, eng="S"):
+            if ("woven", which, h, a) not in tiles:
+                woven_tile(("woven", which, h, a))
+            dst = tiles["woven", which, h, a][:].bitcast(F32)
+            copy(eng, dst[:, b * W:(b + 1) * W].rearrange("p (t r u) -> p t r u", t=2, u=2),
+                 tiles["T", which, h, a, b][:].rearrange("p (t u r) -> p t r u", t=2, u=2))
+            emptied(("T", which, h, a, b))
+
+        def turn(which, h, a, eng="SS"):
+            turn_pe(which, h, a)
+            for b in range(2):
+                turn_out(which, h, a, b, eng[b])
+
+        def quantise(key, tag, bufs, cols=slice(0, W)):
+            if ("codes",) + key not in tiles:
+                tiles[("codes",) + key] = work.tile([P, W], U32, name=tag + "_codes", tag=tag + "_codes", bufs=bufs, align_bytes=64)
+                tiles[("scales",) + key] = work.tile([P, W], U8, name=tag + "_scales", tag=tag + "_scales", bufs=bufs, align_bytes=64)
+            nc.vector.quantize_mx(
+                out=tiles[("codes",) + key][:, cols].bitcast(FP8X4),
+                scales=tiles[("scales",) + key][:, cols],
+                in_=tiles[("woven",) + key][:, cols.start * PACK:cols.stop * PACK],
+            )
+
+        def quant_rows(which, h, a):
+            quantise((which, h, a), "kept", 8)
+
+        def weave(key, src, eng, cols):
+            if ("woven",) + key not in tiles:
+                woven_tile(("woven",) + key)
+            dst = tiles[("woven",) + key][:, cols.start * PACK:cols.stop * PACK]
+            copy(eng, dst.rearrange("p (c i t) -> p c t i", i=4, t=PACK),
+                 src[:, :, cols].rearrange("p t (c i) -> p c t i", i=4))
+
+        def part_cols(part):
+            return slice(0, W) if part is None else slice(part * 256, (part + 1) * 256)
+
+        def weave_x(g, a, eng="V", part=None):
+            weave(("x", g, a), tiles["raw", "x", g, a], eng, part_cols(part))
+
+        def quant_x(g, a):
+            quantise(("x", g, a), "x", 9)
+
+        def mx_pass(bank, left, cols, right, start, stop):
+            nc.tensor.matmul_mx(
+                out=bank[:],
+                lhsT=tiles[("codes",) + left][:, cols].bitcast(FP8X4),
+                lhsT_scale=tiles[("scales",) + left][:, cols],
+                rhs=tiles[("codes",) + right][:].bitcast(FP8X4),
+                rhs_scale=tiles[("scales",) + right][:],
+                start=start, stop=stop,
+            )
+
+        def sums_pass(g, h, t, a):
+            if a == 0:
+                new_bank(("sums", g, h, t))
+            mx_pass(tiles["sums", g, h, t], ("n", h, a), slice(t * P, (t + 1) * P), ("x", g, a), a == 0, a == 2)
+
+        def sums_out(g, h, t, eng="S"):
+            if ("means", g, h) not in tiles:
+                tiles["means", g, h] = work.tile([P, PACK, W], BF16, name="means", tag="means", bufs=4, align_bytes=64)
+            dst = tiles["means", g, h][:, t, :].rearrange("p (j m) -> p j m", j=PACK)
+            src = tiles["sums", g, h, t][:].rearrange("p (m j) -> p j m", j=PACK)
+            if eng == "S":
+                nc.scalar.activation(out=dst, in_=src, func=ACT.Copy, scale=inv_total[:, h, t:t + 1])
+            else:
+                nc.vector.tensor_scalar(out=dst, in0=src, scalar1=inv_total[:, h, t:t + 1], scalar2=None, op0=mybir.AluOpType.mult)
+            emptied(("sums", g, h, t))
+
+        def sums(g, h, eng="SSSS"):
+            for t in range(PACK):
+                for a in range(3):
+                    sums_pass(g, h, t, a)
+                sums_out(g, h, t, eng[t])
+
+        def weave_m(g, h, part=None):
+            weave(("m", g, h), tiles["means", g, h], "V", part_cols(part))
+
+        def quant_m(g, h, part=None):
+            quantise(("m", g, h), "m", 4, part_cols(part))
+
+        def diff_pass(g, j, h):
+            if h == 0:
+                new_bank(("diff", g, j))
+            mx_pass(tiles["diff", g, j], ("m", g, h), slice(j * P, (j + 1) * P), ("c", 0, h), h == 0, h == 1)
+
+        def diff_out(g, j, part=None):
+            cols = part_cols(part)
+            if ("y", g) not in tiles:
+                tiles["y", g] = work.tile([P, PACK, W], F32, name="y_turned", tag="y_turned", bufs=2, align_bytes=64)
+            nc.scalar.activation(out=tiles["y", g][:, j, cols], in_=tiles["diff", g, j][:, cols], func=ACT.Square, scale=root_w[:, g, j:j + 1])
+            if cols.stop == W:
+                emptied(("diff", g, j))
+
+        def diff(g):
+            for j in range(PACK):
+                for h in range(2):
+                    diff_pass(g, j, h)
+                diff_out(g, j)
+
+        def weave_y(g, part=None):
+            weave(("y", g), tiles["y", g], "V", part_cols(part))
+
+        def quant_y(g, part=None):
+            cols = part_cols(part)
+            nc.vector.quantize_mx(out=y_codes[:, g, cols].bitcast(FP8X4), scales=y_scales[:, g, cols], in_=tiles["woven", "y", g][:, cols.start * PACK:cols.stop * PACK])
+            nc.sync.dma_start(out=out_1[g, :, cols, :].rearrange("p m t -> p (m t)").bitcast(I32), in_=y_codes[:, g, cols].bitcast(I32))
+
+        def turn_y_pe(g, i):
+            bank = new_bank(("back", g, i))
+            for j in range(PACK):
+                nc.tensor.transpose(bank[:, j * P:(j + 1) * P], tiles["y", g][:, j, i * P:(i + 1) * P], ident[:])
+
+        def turn_y_out(g, i, eng="S"):
+            rows = work.tile([P, W], F32, name="y_rows", tag="y_rows", bufs=8, align_bytes=64)
+            copy(eng, rows[:].rearrange("c (p j) -> c p j", j=PACK), tiles["back", g, i][:].rearrange("c (j p) -> c p j", j=PACK))
+            emptied(("back", g, i))
+            nc.sync.dma_start(out=out_0[i * P:(i + 1) * P, g * W:(g + 1) * W], in_=rows[:])
+
+        def turn_y(g, eng="SSSS"):
+            for i in range(4):
+                turn_y_pe(g, i)
+            for i in range(4):
+                turn_y_out(g, i, eng[i])
+
+        def store_scales():
+            for q in range(4):
+                nc.sync.dma_start(
+                    out=out_2[:, 4 * q:4 * q + 4, :].rearrange("g r m -> r g m").bitcast(I32),
+                    in_=y_scales[32 * q:32 * q + 4, :, :].bitcast(I32),
+                )
+
+
+        load_small()
+        for h, a in ((0, 0), (0, 1)):
+            load_rows("n", h, a)
+        load_x(0, 0)
+        load_rows("n", 0, 2)
+        load_x(0, 1)
+        load_rows("n", 1, 0)
+        load_x(0, 2)
+        load_rows("n", 1, 1)
+        load_rows("n", 1, 2)
+        for a in range(3):
+            load_x(1, a)
+        for h in range(2):
+            load_rows("c", 0, h)
+        for g in (2, 3):
+            for a in range(3):
+                load_x(g, a)
+
+        def across(g, h, a):
+            for t in range(4):
+                sums_pass(g, h, t, a)
+
+        turn("n", 0, 0)
+        turn("n", 0, 1)
+        quant_rows("n", 0, 0)
+        weave_x(0, 0)
+        quant_rows("n", 0, 1)
+        quant_x(0, 0)
+        turn("n", 0, 2)
+        across(0, 0, 0)
+        weave_x(0, 1)
+        quant_rows("n", 0, 2)
+        quant_x(0, 1)
+        turn("n", 1, 0)
+        across(0, 0, 1)
+        weave_x(0, 2)
+        quant_rows("n", 1, 0)
+        quant_x(0, 2)
+        turn("n", 1, 1)
+        across(0, 0, 2)
+        quant_rows("n", 1, 1)
+        weave_x(1, 0)
+        sums_out(0, 0, 0)
+        sums_out(0, 0, 1)
+        turn("n", 1, 2)
+        sums_out(0, 0, 2)
+        sums_out(0, 0, 3)
+        weave_x(1, 1)
+        across(0, 1, 0)
+        across(0, 1, 1)
+        quant_rows("n", 1, 2)
+        quant_x(1, 0)
+        weave_x(1, 2)
+        quant_x(1, 1)
+        across(0, 1, 2)
+        weave_m(0, 0)
+        quant_x(1, 2)
+        sums_out(0, 1, 0)
+        sums_out(0, 1, 1)
+        turn("c", 0, 0)
+        sums_out(0, 1, 2)
+        sums_out(0, 1, 3)
+        turn("c", 0, 1)
+        weave_x(2, 0)
+        quant_m(0, 0)
+        for g in range(1, 4):
+            more = g < 3
+            sums(g, 0)
+            weave_m(g - 1, 1)
+            if g == 1:
+                quant_rows("c", 0, 0)
+                quant_rows("c", 0, 1)
+            else:
+                quant_m(g - 1, 0)
+                turn_y(g - 2)
+            if more:
+                weave_x(g + 1, 1)
+            quant_m(g - 1, 1)
+            if more:
+                quant_x(g + 1, 0)
+                weave_x(g + 1, 2)
+                quant_x(g + 1, 1)
+            if g > 1:
+                weave_y(g - 2)
+            if more:
+                quant_x(g + 1, 2)
+            sums(g, 1)
+            weave_m(g, 0)
+            if g > 1:
+                quant_y(g - 2)
+            if g == 1:
+                weave_x(3, 0)
+            diff(g - 1)
+        quant_m(3, 0)
+        weave_m(3, 1)
+        for j in range(4):
+            diff_pass(3, j, 0)
+        quant_m(3, 1)
+        weave_y(2)
+        for i in range(4):
+            turn_y_pe(2, i)
+        for j in range(4):
+            diff_pass(3, j, 1)
+        turn_y_out(2, 0, "S")
+        turn_y_out(2, 1, "V")
+        quant_y(2)
+        for j in range(4):
+            diff_out(3, j, 0)
+        turn_y_out(2, 2, "V")
+        turn_y_out(2, 3, "V")
+        for j in range(4):
+            diff_out(3, j, 1)
+        turn_y_pe(3, 0)
+        turn_y_pe(3, 1)
+        weave_y(3, 0)
+        turn_y_out(3, 0, "V")
+        turn_y_pe(3, 2)
+        turn_y_pe(3, 3)
+        quant_y(3, 0)
+        weave_y(3, 1)
+        turn_y_out(3, 1, "S")
+        turn_y_out(3, 2, "S")
+        quant_y(3, 1)
+        store_scales()
+        turn_y_out(3, 3, "S")

@@ -57,40 +57,87 @@ def tile_resampled_contrast_squares_h3_kernel(tc, counts, outcomes, totals, cont
         y_codes = keep.tile([P, 4, W], U32, align_bytes=64)
         y_scales = keep.tile([P, 4, W], U8, align_bytes=64)
 
-        def load_small():
-            nc.scalar.dma_start(out=w_raw[:, :, 0:PACK], in_=study_weights.rearrange("(g p t) -> p g t", p=P, t=PACK))
-            nc.scalar.dma_start(out=tot_raw[:, :, 0:PACK], in_=totals.rearrange("(h p t) -> p h t", p=P, t=PACK))
-            nc.scalar.activation(out=root_w[:], in_=w_raw[:, :, 0:PACK], func=ACT.Sqrt)
-            nc.vector.reciprocal(out=inv_total[:], in_=tot_raw[:, :, 0:PACK])
+        ones = keep.tile([P, W], BF16, align_bytes=64)
+        warm_codes = keep.tile([P, P], U32, align_bytes=64)
+        warm_scales = keep.tile([P, P], U8, align_bytes=64)
+        warm_root = keep.tile([P, 1], F32)
 
-        def raw_tile(key):
-            tiles[key] = work.tile([P, PACK, W], BF16, name="raw", tag="raw", bufs=12, align_bytes=64)
-            return tiles[key]
+        def prepare_warm():
+            nc.vector.memset(ones[:], 1.0)
+            nc.scalar.activation(out=warm_root[:], in_=ones[:, 0:1], func=ACT.Sqrt)
+            nc.vector.quantize_mx(out=warm_codes[:].bitcast(FP8X4), scales=warm_scales[:], in_=ones[:])
+
+        def warm(count):
+            key = ("warm", len(bank_of))
+            bank = new_bank(key)
+            for i in range(count):
+                nc.tensor.matmul_mx(
+                    out=bank[:, (i % 4) * P:(i % 4 + 1) * P],
+                    lhsT=warm_codes[:].bitcast(FP8X4), lhsT_scale=warm_scales[:],
+                    rhs=warm_codes[:].bitcast(FP8X4), rhs_scale=warm_scales[:], start=True, stop=True)
+            emptied(key)
+
+        def load_w(queue=nc.sync):
+            queue.dma_start(out=w_raw[:, :, 0:PACK], in_=study_weights.rearrange("(g p t) -> p g t", p=P, t=PACK))
+
+        def load_tot():
+            nc.sync.dma_start(out=tot_raw[:, :, 0:PACK], in_=totals.rearrange("(h p t) -> p h t", p=P, t=PACK))
+
+        def root():
+            nc.scalar.activation(out=root_w[:], in_=w_raw[:, :, 0:PACK], func=ACT.Sqrt)
+
+        def recip():
+            nc.vector.reciprocal(out=inv_total[:], in_=tot_raw[:, :, 0:PACK])
 
         def woven_tile(key):
             tiles[key] = work.tile([P, W * PACK], BF16, name="woven", tag="woven", bufs=8, align_bytes=64)
             return tiles[key]
 
-        def load_rows(which, h, a):
-            raw = raw_tile(("raw", which, h, a))
+        segment = {}
+
+        def load_rows(which, h, piece):
             if which == "n":
-                src = counts[h * W:(h + 1) * W, a * W:(a + 1) * W].rearrange("(m t) k -> m t k", t=PACK)
+                rows = counts[h * W:(h + 1) * W, :].rearrange("(m t) k -> m t k", t=PACK)
             else:
-                src = contrasts[:, a * W:(a + 1) * W].rearrange("(t m) k -> m t k", t=PACK)
-            nc.sync.dma_start(out=raw[:], in_=src)
+                rows = contrasts.rearrange("(t m) k -> m t k", t=PACK)
+            passes = list(range(rows.shape[2] // W))
+            slots = [0, 1, 2, 3] if piece == "a" else [2 * piece, 2 * piece + 1]
+            if (which, h) == ("n", 0):
+                passes = [0] if piece == "a" else [1, 2]
+            name = "raw_%s%d%s" % (which, h, piece)
+            raw = keep.tile([P, len(slots), len(passes) * W], BF16, name=name, tag=name, align_bytes=64)
+            nc.sync.dma_start(out=raw[:], in_=rows[:, slots[0]:slots[-1] + 1, passes[0] * W:(passes[-1] + 1) * W])
+            tiles["piece", which, h, piece] = raw[:].rearrange("m t k -> m (t k)").bitcast(F32)
+            for i, t in enumerate(slots):
+                for j, a in enumerate(passes):
+                    segment[which, h, a, t] = (piece, (i * len(passes) + j) * 256)
+
+        def shuffle(which, h, piece, eng):
+            words = tiles["piece", which, h, piece]
+            name = "sorted_%s%d%s" % (which, h, piece)
+            out = keep.tile([P, words.shape[1]], F32, name=name, tag=name, align_bytes=64)
+            copy(eng, out[:].rearrange("m (s u p) -> m s u p", u=2, p=P), words.rearrange("m (s p u) -> m s u p", u=2, p=P))
+            tiles["sorted", which, h, piece] = out
 
         def load_x(g, a):
-            raw = raw_tile(("raw", "x", g, a))
-            src = outcomes[a * W:(a + 1) * W, g * W:(g + 1) * W].rearrange("(p j) s -> p j s", j=PACK)
+            width = W if g < 2 else 2 * W
+            tag = "raw_x%d" % width
+            raw = work.tile([P, PACK, width], BF16, name=tag, tag=tag, bufs=3 if g == 2 else 6, align_bytes=64)
+            src = outcomes[a * W:(a + 1) * W, g * W:g * W + width].rearrange("(p j) s -> p j s", j=PACK)
             nc.sync.dma_start(out=raw[:], in_=src)
+            for i in range(width // W):
+                tiles["raw", "x", g + i, a] = raw[:, :, i * W:(i + 1) * W]
 
-        def turn_pe(which, h, a):
-            words = tiles["raw", which, h, a][:].rearrange("m t k -> m (t k)").bitcast(F32)
-            for b in range(2):
-                bank = new_bank(("T", which, h, a, b))
-                for i in range(4):
-                    t, u = 2 * b + i // 2, i % 2
-                    nc.tensor.transpose(bank[:, i * P:(i + 1) * P], words[:, 256 * t + u:256 * (t + 1):2], ident[:])
+        def turn_pe(which, h, a, b):
+            bank = new_bank(("T", which, h, a, b))
+            for i in range(4):
+                t, u = 2 * b + i // 2, i % 2
+                piece, start = segment[which, h, a, t]
+                if ("sorted", which, h, piece) in tiles:
+                    words = tiles["sorted", which, h, piece][:, start + u * P:start + (u + 1) * P]
+                else:
+                    words = tiles["piece", which, h, piece][:, start + u:start + 256:2]
+                nc.tensor.transpose(bank[:, i * P:(i + 1) * P], words, ident[:])
 
         def turn_out(which, h, a, b, eng="S"):
             if ("woven", which, h, a) not in tiles:
@@ -101,7 +148,8 @@ def tile_resampled_contrast_squares_h3_kernel(tc, counts, outcomes, totals, cont
             emptied(("T", which, h, a, b))
 
         def turn(which, h, a, eng="SS"):
-            turn_pe(which, h, a)
+            for b in range(2):
+                turn_pe(which, h, a, b)
             for b in range(2):
                 turn_out(which, h, a, b, eng[b])
 
@@ -115,8 +163,8 @@ def tile_resampled_contrast_squares_h3_kernel(tc, counts, outcomes, totals, cont
                 in_=tiles[("woven",) + key][:, cols.start * PACK:cols.stop * PACK],
             )
 
-        def quant_rows(which, h, a):
-            quantise((which, h, a), "kept", 8)
+        def quant_rows(which, h, a, part=None):
+            quantise((which, h, a), "kept", 8, part_cols(part))
 
         def weave(key, src, eng, cols):
             if ("woven",) + key not in tiles:
@@ -216,100 +264,102 @@ def tile_resampled_contrast_squares_h3_kernel(tc, counts, outcomes, totals, cont
             for i in range(4):
                 turn_y_out(g, i, eng[i])
 
-        def store_scales():
+        def store_scales(last):
+            groups = slice(3, 4) if last else slice(0, 3)
             for q in range(4):
                 nc.sync.dma_start(
-                    out=out_2[:, 4 * q:4 * q + 4, :].rearrange("g r m -> r g m").bitcast(I32),
-                    in_=y_scales[32 * q:32 * q + 4, :, :].bitcast(I32),
+                    out=out_2[groups, 4 * q:4 * q + 4, :].rearrange("g r m -> r g m").bitcast(I32),
+                    in_=y_scales[32 * q:32 * q + 4, groups, :].bitcast(I32),
                 )
 
 
-        load_small()
-        for h, a in ((0, 0), (0, 1)):
-            load_rows("n", h, a)
+        prepare_warm()
+        load_rows("n", 0, "a")
+        load_rows("n", 0, 0)
         load_x(0, 0)
-        load_rows("n", 0, 2)
+        load_rows("n", 0, 1)
         load_x(0, 1)
         load_rows("n", 1, 0)
         load_x(0, 2)
         load_rows("n", 1, 1)
-        load_rows("n", 1, 2)
+        load_tot()
         for a in range(3):
             load_x(1, a)
-        for h in range(2):
-            load_rows("c", 0, h)
-        for g in (2, 3):
-            for a in range(3):
-                load_x(g, a)
+        for b in range(2):
+            load_rows("c", 0, b)
+        load_w()
+        for a in range(3):
+            load_x(2, a)
 
         def across(g, h, a):
             for t in range(4):
                 sums_pass(g, h, t, a)
 
+        def turn_piece(which, h, b, passes):
+            for a in passes:
+                turn_pe(which, h, a, b)
+            for a in passes:
+                turn_out(which, h, a, b)
+
+        warm(18)
         turn("n", 0, 0)
-        turn("n", 0, 1)
+        warm(8)
+        turn_piece("n", 0, 0, (1, 2))
+        warm(14)
         quant_rows("n", 0, 0)
         weave_x(0, 0)
-        quant_rows("n", 0, 1)
         quant_x(0, 0)
-        turn("n", 0, 2)
+        turn_piece("n", 0, 1, (1, 2))
         across(0, 0, 0)
         weave_x(0, 1)
-        quant_rows("n", 0, 2)
+        quant_rows("n", 0, 1)
         quant_x(0, 1)
-        turn("n", 1, 0)
+        quant_rows("n", 0, 2)
+        turn_piece("n", 1, 0, (0, 1, 2))
         across(0, 0, 1)
         weave_x(0, 2)
-        quant_rows("n", 1, 0)
+        for a in range(3):
+            quant_rows("n", 1, a, 0)
         quant_x(0, 2)
-        turn("n", 1, 1)
+        turn_piece("n", 1, 1, (0, 1, 2))
         across(0, 0, 2)
-        quant_rows("n", 1, 1)
+        recip()
+        for a in range(3):
+            quant_rows("n", 1, a, 1)
         weave_x(1, 0)
-        sums_out(0, 0, 0)
-        sums_out(0, 0, 1)
-        turn("n", 1, 2)
-        sums_out(0, 0, 2)
-        sums_out(0, 0, 3)
+        for t in range(4):
+            sums_out(0, 0, t)
+        sums(0, 1)
         weave_x(1, 1)
-        across(0, 1, 0)
-        across(0, 1, 1)
-        quant_rows("n", 1, 2)
         quant_x(1, 0)
         weave_x(1, 2)
         quant_x(1, 1)
-        across(0, 1, 2)
         weave_m(0, 0)
         quant_x(1, 2)
-        sums_out(0, 1, 0)
-        sums_out(0, 1, 1)
-        turn("c", 0, 0)
-        sums_out(0, 1, 2)
-        sums_out(0, 1, 3)
-        turn("c", 0, 1)
-        weave_x(2, 0)
+        turn_piece("c", 0, 0, (0, 1))
+        turn_piece("c", 0, 1, (0, 1))
+        weave_m(0, 1)
         quant_m(0, 0)
-        for g in range(1, 4):
-            more = g < 3
+        for g in range(1, 3):
             sums(g, 0)
-            weave_m(g - 1, 1)
+            if g == 1:
+                root()
             if g == 1:
                 quant_rows("c", 0, 0)
                 quant_rows("c", 0, 1)
+                weave_x(2, 0)
             else:
+                weave_m(g - 1, 1)
                 quant_m(g - 1, 0)
                 turn_y(g - 2)
-            if more:
-                weave_x(g + 1, 1)
+            weave_x(g + 1, 1)
             quant_m(g - 1, 1)
-            if more:
-                quant_x(g + 1, 0)
-                weave_x(g + 1, 2)
-                quant_x(g + 1, 1)
+            quant_x(g + 1, 0)
+            weave_x(g + 1, 2)
+            quant_x(g + 1, 1)
             if g > 1:
                 weave_y(g - 2)
-            if more:
-                quant_x(g + 1, 2)
+            quant_x(g + 1, 2)
             sums(g, 1)
             weave_m(g, 0)
             if g > 1:
@@ -317,35 +367,47 @@ def tile_resampled_contrast_squares_h3_kernel(tc, counts, outcomes, totals, cont
             if g == 1:
                 weave_x(3, 0)
             diff(g - 1)
+        sums(3, 0)
+        weave_m(2, 1)
+        quant_m(2, 0)
+        weave_y(1)
+        quant_m(2, 1)
+        turn_y(1)
+        sums(3, 1)
+        weave_m(3, 0)
+        quant_y(1)
+        diff(2)
         quant_m(3, 0)
-        weave_m(3, 1)
+        weave_m(3, 1, 0)
+        weave_m(3, 1, 1)
+        quant_m(3, 1, 0)
+        quant_m(3, 1, 1)
         for j in range(4):
             diff_pass(3, j, 0)
-        quant_m(3, 1)
-        weave_y(2)
         for i in range(4):
             turn_y_pe(2, i)
         for j in range(4):
             diff_pass(3, j, 1)
+        weave_y(2)
         turn_y_out(2, 0, "S")
-        turn_y_out(2, 1, "V")
-        quant_y(2)
-        for j in range(4):
-            diff_out(3, j, 0)
+        turn_y_out(2, 1, "S")
         turn_y_out(2, 2, "V")
+        quant_y(2)
         turn_y_out(2, 3, "V")
-        for j in range(4):
-            diff_out(3, j, 1)
+        store_scales(False)
+        for part in range(2):
+            for j in range(4):
+                diff_out(3, j, part)
         turn_y_pe(3, 0)
         turn_y_pe(3, 1)
         weave_y(3, 0)
-        turn_y_out(3, 0, "V")
+        turn_y_out(3, 0, "S")
         turn_y_pe(3, 2)
         turn_y_pe(3, 3)
-        quant_y(3, 0)
         weave_y(3, 1)
         turn_y_out(3, 1, "S")
-        turn_y_out(3, 2, "S")
+        quant_y(3, 0)
         quant_y(3, 1)
-        store_scales()
+        turn_y_out(3, 2, "S")
         turn_y_out(3, 3, "S")
+        store_scales(True)

@@ -200,8 +200,8 @@ def tile_resampled_contrast_squares_h3_kernel(tc, counts, outcomes, totals, cont
         def sums_out(g, h, t, eng="S"):
             if ("means", g, h) not in tiles:
                 tiles["means", g, h] = work.tile([P, PACK, W], BF16, name="means", tag="means", bufs=4, align_bytes=64)
-            dst = tiles["means", g, h][:, t, :].rearrange("p (j m) -> p j m", j=PACK)
-            src = tiles["sums", g, h, t][:].rearrange("p (m j) -> p j m", j=PACK)
+            dst = tiles["means", g, h][:, t, :]
+            src = tiles["sums", g, h, t][:]
             if eng == "S":
                 nc.scalar.activation(out=dst, in_=src, func=ACT.Copy, scale=inv_total[:, h, t:t + 1])
             else:
@@ -215,7 +215,13 @@ def tile_resampled_contrast_squares_h3_kernel(tc, counts, outcomes, totals, cont
                 sums_out(g, h, t, eng[t])
 
         def weave_m(g, h, part=None):
-            weave(("m", g, h), tiles["means", g, h], "V", part_cols(part))
+            if ("woven", "m", g, h) not in tiles:
+                woven_tile(("woven", "m", g, h))
+            js = slice(0, PACK) if part is None else slice(2 * part, 2 * part + 2)
+            nc.vector.tensor_copy(
+                out=tiles["woven", "m", g, h][:].rearrange("p (j m t) -> p m t j", j=PACK, t=PACK)[:, :, :, js],
+                in_=tiles["means", g, h][:].rearrange("p t (m j) -> p m t j", j=PACK)[:, :, :, js],
+            )
 
         def quant_m(g, h, part=None):
             quantise(("m", g, h), "m", 4, part_cols(part))
@@ -265,7 +271,7 @@ def tile_resampled_contrast_squares_h3_kernel(tc, counts, outcomes, totals, cont
                 turn_y_out(g, i, eng[i])
 
         def store_scales(last):
-            groups = slice(3, 4) if last else slice(0, 3)
+            groups = slice(2, 4) if last else slice(0, 2)
             for q in range(4):
                 nc.sync.dma_start(
                     out=out_2[groups, 4 * q:4 * q + 4, :].rearrange("g r m -> r g m").bitcast(I32),
@@ -324,9 +330,9 @@ def tile_resampled_contrast_squares_h3_kernel(tc, counts, outcomes, totals, cont
         turn_piece("n", 1, 1, (0, 1, 2))
         across(0, 0, 2)
         recip()
+        weave_x(1, 0)
         for a in range(3):
             quant_rows("n", 1, a, 1)
-        weave_x(1, 0)
         for t in range(4):
             sums_out(0, 0, t)
         sums(0, 1)
@@ -334,8 +340,8 @@ def tile_resampled_contrast_squares_h3_kernel(tc, counts, outcomes, totals, cont
         quant_x(1, 0)
         weave_x(1, 2)
         quant_x(1, 1)
-        weave_m(0, 0)
         quant_x(1, 2)
+        weave_m(0, 0)
         turn_piece("c", 0, 0, (0, 1))
         turn_piece("c", 0, 1, (0, 1))
         weave_m(0, 1)
@@ -357,9 +363,9 @@ def tile_resampled_contrast_squares_h3_kernel(tc, counts, outcomes, totals, cont
             quant_x(g + 1, 0)
             weave_x(g + 1, 2)
             quant_x(g + 1, 1)
+            quant_x(g + 1, 2)
             if g > 1:
                 weave_y(g - 2)
-            quant_x(g + 1, 2)
             sums(g, 1)
             weave_m(g, 0)
             if g > 1:
@@ -373,11 +379,12 @@ def tile_resampled_contrast_squares_h3_kernel(tc, counts, outcomes, totals, cont
         weave_y(1)
         quant_m(2, 1)
         turn_y(1)
-        sums(3, 1)
         weave_m(3, 0)
         quant_y(1)
-        diff(2)
+        store_scales(False)
         quant_m(3, 0)
+        sums(3, 1, "SSSV")
+        diff(2)
         weave_m(3, 1, 0)
         weave_m(3, 1, 1)
         quant_m(3, 1, 0)
@@ -394,7 +401,6 @@ def tile_resampled_contrast_squares_h3_kernel(tc, counts, outcomes, totals, cont
         turn_y_out(2, 2, "V")
         quant_y(2)
         turn_y_out(2, 3, "V")
-        store_scales(False)
         for part in range(2):
             for j in range(4):
                 diff_out(3, j, part)

@@ -39,6 +39,9 @@ def tile_resampled_contrast_squares_h3_kernel(tc, counts, outcomes, totals, cont
             tiles[key] = psum.tile([P, W], F32, name=tag, tag=tag)
             return tiles[key]
 
+        def newest_first():
+            idle[:PACK] = reversed(idle[:PACK])
+
         def emptied(key):
             idle.append(bank_of[key])
 
@@ -56,26 +59,6 @@ def tile_resampled_contrast_squares_h3_kernel(tc, counts, outcomes, totals, cont
         root_w = keep.tile([P, 4, PACK], F32)
         y_codes = keep.tile([P, 4, W], U32, align_bytes=64)
         y_scales = keep.tile([P, 4, W], U8, align_bytes=64)
-
-        ones = keep.tile([P, W], BF16, align_bytes=64)
-        warm_codes = keep.tile([P, P], U32, align_bytes=64)
-        warm_scales = keep.tile([P, P], U8, align_bytes=64)
-        warm_root = keep.tile([P, 1], F32)
-
-        def prepare_warm():
-            nc.vector.memset(ones[:], 1.0)
-            nc.scalar.activation(out=warm_root[:], in_=ones[:, 0:1], func=ACT.Sqrt)
-            nc.vector.quantize_mx(out=warm_codes[:].bitcast(FP8X4), scales=warm_scales[:], in_=ones[:])
-
-        def warm(count):
-            key = ("warm", len(bank_of))
-            bank = new_bank(key)
-            for i in range(count):
-                nc.tensor.matmul_mx(
-                    out=bank[:, (i % 4) * P:(i % 4 + 1) * P],
-                    lhsT=warm_codes[:].bitcast(FP8X4), lhsT_scale=warm_scales[:],
-                    rhs=warm_codes[:].bitcast(FP8X4), rhs_scale=warm_scales[:], start=True, stop=True)
-            emptied(key)
 
         def load_w(queue=nc.sync):
             queue.dma_start(out=w_raw[:, :, 0:PACK], in_=study_weights.rearrange("(g p t) -> p g t", p=P, t=PACK))
@@ -209,6 +192,8 @@ def tile_resampled_contrast_squares_h3_kernel(tc, counts, outcomes, totals, cont
             emptied(("sums", g, h, t))
 
         def sums(g, h, eng="SSSS"):
+            if g > 0:
+                newest_first()
             for t in range(PACK):
                 for a in range(3):
                     sums_pass(g, h, t, a)
@@ -240,6 +225,7 @@ def tile_resampled_contrast_squares_h3_kernel(tc, counts, outcomes, totals, cont
                 emptied(("diff", g, j))
 
         def diff(g):
+            newest_first()
             for j in range(PACK):
                 for h in range(2):
                     diff_pass(g, j, h)
@@ -265,6 +251,7 @@ def tile_resampled_contrast_squares_h3_kernel(tc, counts, outcomes, totals, cont
             nc.sync.dma_start(out=out_0[i * P:(i + 1) * P, g * W:(g + 1) * W], in_=rows[:])
 
         def turn_y(g, eng="SSSS"):
+            newest_first()
             for i in range(4):
                 turn_y_pe(g, i)
             for i in range(4):
@@ -279,10 +266,11 @@ def tile_resampled_contrast_squares_h3_kernel(tc, counts, outcomes, totals, cont
                 )
 
 
-        prepare_warm()
+        load_w(nc.scalar)
+        root()
         load_rows("n", 0, "a")
-        load_rows("n", 0, 0)
         load_x(0, 0)
+        load_rows("n", 0, 0)
         load_rows("n", 0, 1)
         load_x(0, 1)
         load_rows("n", 1, 0)
@@ -293,7 +281,6 @@ def tile_resampled_contrast_squares_h3_kernel(tc, counts, outcomes, totals, cont
             load_x(1, a)
         for b in range(2):
             load_rows("c", 0, b)
-        load_w()
         for a in range(3):
             load_x(2, a)
 
@@ -307,16 +294,13 @@ def tile_resampled_contrast_squares_h3_kernel(tc, counts, outcomes, totals, cont
             for a in passes:
                 turn_out(which, h, a, b)
 
-        warm(18)
         turn("n", 0, 0)
-        warm(8)
-        turn_piece("n", 0, 0, (1, 2))
-        warm(14)
-        quant_rows("n", 0, 0)
         weave_x(0, 0)
+        quant_rows("n", 0, 0)
         quant_x(0, 0)
-        turn_piece("n", 0, 1, (1, 2))
+        turn_piece("n", 0, 0, (1, 2))
         across(0, 0, 0)
+        turn_piece("n", 0, 1, (1, 2))
         weave_x(0, 1)
         quant_rows("n", 0, 1)
         quant_x(0, 1)
@@ -348,8 +332,6 @@ def tile_resampled_contrast_squares_h3_kernel(tc, counts, outcomes, totals, cont
         quant_m(0, 0)
         for g in range(1, 3):
             sums(g, 0)
-            if g == 1:
-                root()
             if g == 1:
                 quant_rows("c", 0, 0)
                 quant_rows("c", 0, 1)

from contextlib import ExitStack

import concourse.mybir as mybir
from concourse.masks import make_identity

U, G, S, C = 1536, 1024, 2048, 512
FLOPS = 2 * G * U * S + 2 * C * G * S

F32 = mybir.dt.float32
BF16 = mybir.dt.bfloat16
U32 = mybir.dt.uint32
I32 = mybir.dt.int32
U8 = mybir.dt.uint8
FP8X4 = mybir.dt.float8_e4m3fn_x4
ACT = mybir.ActivationFunctionType

P = 128
PACK = 4
W = 512
BANKS = 8


def tile_resampled_contrast_squares_h3_kernel(tc, counts, outcomes, totals, contrasts, study_weights, out_0, out_1, out_2):
    nc = tc.nc
    with ExitStack() as ctx:
        keep = ctx.enter_context(tc.tile_pool(name="keep", bufs=1))
        work = ctx.enter_context(tc.tile_pool(name="work", bufs=1))
        psum = ctx.enter_context(tc.psum_pool(name="psum", bufs=1))
        ctx.enter_context(tc.manual_schedule())

        tiles = {}
        idle = list(range(BANKS))
        bank_of = {}

        def new_bank(key):
            bank_of[key] = idle[0]
            idle.remove(bank_of[key])
            tag = "bank%d" % bank_of[key]
            tiles[key] = psum.tile([P, W], F32, name=tag, tag=tag)
            return tiles[key]

        def newest_first():
            idle[:PACK] = reversed(idle[:PACK])

        def emptied(key):
            idle.append(bank_of[key])

        def copy(eng, out, in_):
            if eng == "S":
                nc.scalar.copy(out=out, in_=in_)
            else:
                nc.vector.tensor_copy(out=out, in_=in_)

        ident = keep.tile([P, P], F32)
        make_identity(nc, ident[:])
        tot_raw = keep.tile([P, 2, 16], BF16)
        w_raw = keep.tile([P, 4, 16], BF16)
        inv_total = keep.tile([P, 2, PACK], F32)
        root_w = keep.tile([P, 4, PACK], F32)
        y_codes = keep.tile([P, 4, W], U32, align_bytes=64)
        y_scales = keep.tile([P, 4, W], U8, align_bytes=64)

        def load_w(queue=nc.sync):
            queue.dma_start(out=w_raw[:, :, 0:PACK], in_=study_weights.rearrange("(g p t) -> p g t", p=P, t=PACK))

        def load_tot():
            nc.sync.dma_start(out=tot_raw[:, :, 0:PACK], in_=totals.rearrange("(h p t) -> p h t", p=P, t=PACK))

        def root():
            nc.scalar.activation(out=root_w[:], in_=w_raw[:, :, 0:PACK], func=ACT.Sqrt)

        def recip():
            nc.vector.reciprocal(out=inv_total[:], in_=tot_raw[:, :, 0:PACK])

        def woven_tile(key):
            tiles[key] = work.tile([P, W * PACK], BF16, name="woven", tag="woven", bufs=8, align_bytes=64)
            return tiles[key]

        segment = {}

        def load_rows(which, h, piece):
            if which == "n":
                rows = counts[h * W:(h + 1) * W, :].rearrange("(m t) k -> m t k", t=PACK)
            else:
                rows = contrasts.rearrange("(t m) k -> m t k", t=PACK)
            passes = list(range(rows.shape[2] // W))
            slots = [0, 1, 2, 3] if piece == "a" else [2 * piece, 2 * piece + 1]
            if (which, h) == ("n", 0):
                passes = [0] if piece == "a" else [1, 2]
            name = "raw_%s%d%s" % (which, h, piece)
            raw = keep.tile([P, len(slots), len(passes) * W], BF16, name=name, tag=name, align_bytes=64)
            nc.sync.dma_start(out=raw[:], in_=rows[:, slots[0]:slots[-1] + 1, passes[0] * W:(passes[-1] + 1) * W])
            tiles["piece", which, h, piece] = raw[:].rearrange("m t k -> m (t k)").bitcast(F32)
            for i, t in enumerate(slots):
                for j, a in enumerate(passes):
                    segment[which, h, a, t] = (piece, (i * len(passes) + j) * 256)

        def shuffle(which, h, piece, eng):
            words = tiles["piece", which, h, piece]
            name = "sorted_%s%d%s" % (which, h, piece)
            out = keep.tile([P, words.shape[1]], F32, name=name, tag=name, align_bytes=64)
            copy(eng, out[:].rearrange("m (s u p) -> m s u p", u=2, p=P), words.rearrange("m (s p u) -> m s u p", u=2, p=P))
            tiles["sorted", which, h, piece] = out

        def load_x(g, a):
            width = W if g < 2 else 2 * W
            tag = "raw_x%d" % width
            raw = work.tile([P, PACK, width], BF16, name=tag, tag=tag, bufs=3 if g == 2 else 6, align_bytes=64)
            src = outcomes[a * W:(a + 1) * W, g * W:g * W + width].rearrange("(p j) s -> p j s", j=PACK)
            nc.sync.dma_start(out=raw[:], in_=src)
            for i in range(width // W):
                tiles["raw", "x", g + i, a] = raw[:, :, i * W:(i + 1) * W]

        def turn_pe(which, h, a, b):
            bank = new_bank(("T", which, h, a, b))
            for i in range(4):
                t, u = 2 * b + i // 2, i % 2
                piece, start = segment[which, h, a, t]
                if ("sorted", which, h, piece) in tiles:
                    words = tiles["sorted", which, h, piece][:, start + u * P:start + (u + 1) * P]
                else:
                    words = tiles["piece", which, h, piece][:, start + u:start + 256:2]
                nc.tensor.transpose(bank[:, i * P:(i + 1) * P], words, ident[:])

        def turn_out(which, h, a, b, eng="S"):
            if ("woven", which, h, a) not in tiles:
                woven_tile(("woven", which, h, a))
            dst = tiles["woven", which, h, a][:].bitcast(F32)
            copy(eng, dst[:, b * W:(b + 1) * W].rearrange("p (t r u) -> p t r u", t=2, u=2),
                 tiles["T", which, h, a, b][:].rearrange("p (t u r) -> p t r u", t=2, u=2))
            emptied(("T", which, h, a, b))

        def turn(which, h, a, eng="SS"):
            for b in range(2):
                turn_pe(which, h, a, b)
            for b in range(2):
                turn_out(which, h, a, b, eng[b])

        def quantise(key, tag, bufs, cols=slice(0, W)):
            if ("codes",) + key not in tiles:
                tiles[("codes",) + key] = work.tile([P, W], U32, name=tag + "_codes", tag=tag + "_codes", bufs=bufs, align_bytes=64)
                tiles[("scales",) + key] = work.tile([P, W], U8, name=tag + "_scales", tag=tag + "_scales", bufs=bufs, align_bytes=64)
            nc.vector.quantize_mx(
                out=tiles[("codes",) + key][:, cols].bitcast(FP8X4),
                scales=tiles[("scales",) + key][:, cols],
                in_=tiles[("woven",) + key][:, cols.start * PACK:cols.stop * PACK],
            )

        def quant_rows(which, h, a, part=None):
            quantise((which, h, a), "kept", 8, part_cols(part))

        def weave(key, src, eng, cols):
            if ("woven",) + key not in tiles:
                woven_tile(("woven",) + key)
            dst = tiles[("woven",) + key][:, cols.start * PACK:cols.stop * PACK]
            copy(eng, dst.rearrange("p (c i t) -> p c t i", i=4, t=PACK),
                 src[:, :, cols].rearrange("p t (c i) -> p c t i", i=4))

        def part_cols(part):
            return slice(0, W) if part is None else slice(part * 256, (part + 1) * 256)

        def weave_x(g, a, eng="V", part=None):
            weave(("x", g, a), tiles["raw", "x", g, a], eng, part_cols(part))

        def quant_x(g, a):
            quantise(("x", g, a), "x", 9)

        def mx_pass(bank, left, cols, right, start, stop):
            nc.tensor.matmul_mx(
                out=bank[:],
                lhsT=tiles[("codes",) + left][:, cols].bitcast(FP8X4),
                lhsT_scale=tiles[("scales",) + left][:, cols],
                rhs=tiles[("codes",) + right][:].bitcast(FP8X4),
                rhs_scale=tiles[("scales",) + right][:],
                start=start, stop=stop,
            )

        def sums_pass(g, h, t, a):
            if a == 0:
                new_bank(("sums", g, h, t))
            mx_pass(tiles["sums", g, h, t], ("n", h, a), slice(t * P, (t + 1) * P), ("x", g, a), a == 0, a == 2)

        def sums_out(g, h, t, eng="S"):
            if ("means", g, h) not in tiles:
                tiles["means", g, h] = work.tile([P, PACK, W], BF16, name="means", tag="means", bufs=4, align_bytes=64)
            dst = tiles["means", g, h][:, t, :]
            src = tiles["sums", g, h, t][:]
            if eng == "S":
                nc.scalar.activation(out=dst, in_=src, func=ACT.Copy, scale=inv_total[:, h, t:t + 1])
            else:
                nc.vector.tensor_scalar(out=dst, in0=src, scalar1=inv_total[:, h, t:t + 1], scalar2=None, op0=mybir.AluOpType.mult)
            emptied(("sums", g, h, t))

        def sums(g, h, eng="SSSS"):
            if g > 0:
                newest_first()
            for t in range(PACK):
                for a in range(3):
                    sums_pass(g, h, t, a)
                sums_out(g, h, t, eng[t])

        def weave_m(g, h, part=None):
            if ("woven", "m", g, h) not in tiles:
                woven_tile(("woven", "m", g, h))
            js = slice(0, PACK) if part is None else slice(2 * part, 2 * part + 2)
            nc.vector.tensor_copy(
                out=tiles["woven", "m", g, h][:].rearrange("p (j m t) -> p m t j", j=PACK, t=PACK)[:, :, :, js],
                in_=tiles["means", g, h][:].rearrange("p t (m j) -> p m t j", j=PACK)[:, :, :, js],
            )

        def quant_m(g, h, part=None):
            quantise(("m", g, h), "m", 4, part_cols(part))

        def diff_pass(g, j, h):
            if h == 0:
                new_bank(("diff", g, j))
            mx_pass(tiles["diff", g, j], ("m", g, h), slice(j * P, (j + 1) * P), ("c", 0, h), h == 0, h == 1)

        def diff_out(g, j, part=None):
            cols = part_cols(part)
            if ("y", g) not in tiles:
                tiles["y", g] = work.tile([P, PACK, W], F32, name="y_turned", tag="y_turned", bufs=2, align_bytes=64)
            nc.scalar.activation(out=tiles["y", g][:, j, cols], in_=tiles["diff", g, j][:, cols], func=ACT.Square, scale=root_w[:, g, j:j + 1])
            if cols.stop == W:
                emptied(("diff", g, j))

        def diff(g):
            newest_first()
            for j in range(PACK):
                for h in range(2):
                    diff_pass(g, j, h)
                diff_out(g, j)

        def weave_y(g, part=None):
            weave(("y", g), tiles["y", g], "V", part_cols(part))

        def quant_y(g, part=None):
            cols = part_cols(part)
            nc.vector.quantize_mx(out=y_codes[:, g, cols].bitcast(FP8X4), scales=y_scales[:, g, cols], in_=tiles["woven", "y", g][:, cols.start * PACK:cols.stop * PACK])
            nc.sync.dma_start(out=out_1[g, :, cols, :].rearrange("p m t -> p (m t)").bitcast(I32), in_=y_codes[:, g, cols].bitcast(I32))

        def turn_y_pe(g, i):
            bank = new_bank(("back", g, i))
            for j in range(PACK):
                nc.tensor.transpose(bank[:, j * P:(j + 1) * P], tiles["y", g][:, j, i * P:(i + 1) * P], ident[:])

        def turn_y_out(g, i, eng="S"):
            rows = work.tile([P, W], F32, name="y_rows", tag="y_rows", bufs=8, align_bytes=64)
            copy(eng, rows[:].rearrange("c (p j) -> c p j", j=PACK), tiles["back", g, i][:].rearrange("c (j p) -> c p j", j=PACK))
            emptied(("back", g, i))
            nc.sync.dma_start(out=out_0[i * P:(i + 1) * P, g * W:(g + 1) * W], in_=rows[:])

        def turn_y(g, eng="SSSS"):
            newest_first()
            for i in range(4):
                turn_y_pe(g, i)
            for i in range(4):
                turn_y_out(g, i, eng[i])

        def store_scales(last):
            groups = slice(2, 4) if last else slice(0, 2)
            for q in range(4):
                nc.sync.dma_start(
                    out=out_2[groups, 4 * q:4 * q + 4, :].rearrange("g r m -> r g m").bitcast(I32),
                    in_=y_scales[32 * q:32 * q + 4, groups, :].bitcast(I32),
                )


        load_w(nc.scalar)
        root()
        load_rows("n", 0, "a")
        load_x(0, 0)
        load_rows("n", 0, 0)
        load_rows("n", 0, 1)
        load_x(0, 1)
        load_rows("n", 1, 0)
        load_x(0, 2)
        load_rows("n", 1, 1)
        load_tot()
        for a in range(3):
            load_x(1, a)
        for b in range(2):
            load_rows("c", 0, b)
        for a in range(3):
            load_x(2, a)

        def across(g, h, a):
            for t in range(4):
                sums_pass(g, h, t, a)

        def turn_piece(which, h, b, passes):
            for a in passes:
                turn_pe(which, h, a, b)
            for a in passes:
                turn_out(which, h, a, b)

        turn("n", 0, 0)
        weave_x(0, 0)
        quant_rows("n", 0, 0)
        quant_x(0, 0)
        turn_piece("n", 0, 0, (1, 2))
        across(0, 0, 0)
        turn_piece("n", 0, 1, (1, 2))
        weave_x(0, 1)
        quant_rows("n", 0, 1)
        quant_x(0, 1)
        quant_rows("n", 0, 2)
        turn_piece("n", 1, 0, (0, 1, 2))
        across(0, 0, 1)
        weave_x(0, 2)
        for a in range(3):
            quant_rows("n", 1, a, 0)
        quant_x(0, 2)
        turn_piece("n", 1, 1, (0, 1, 2))
        across(0, 0, 2)
        recip()
        weave_x(1, 0)
        for a in range(3):
            quant_rows("n", 1, a, 1)
        for t in range(4):
            sums_out(0, 0, t)
        sums(0, 1)
        weave_x(1, 1)
        quant_x(1, 0)
        weave_x(1, 2)
        quant_x(1, 1)
        quant_x(1, 2)
        weave_m(0, 0)
        turn_piece("c", 0, 0, (0, 1))
        turn_piece("c", 0, 1, (0, 1))
        weave_m(0, 1)
        quant_m(0, 0)
        for g in range(1, 3):
            sums(g, 0)
            if g == 1:
                quant_rows("c", 0, 0)
                quant_rows("c", 0, 1)
                weave_x(2, 0)
            else:
                weave_m(g - 1, 1)
                quant_m(g - 1, 0)
                turn_y(g - 2)
            weave_x(g + 1, 1)
            quant_m(g - 1, 1)
            quant_x(g + 1, 0)
            weave_x(g + 1, 2)
            quant_x(g + 1, 1)
            quant_x(g + 1, 2)
            if g > 1:
                weave_y(g - 2)
            sums(g, 1)
            weave_m(g, 0)
            if g > 1:
                quant_y(g - 2)
            if g == 1:
                weave_x(3, 0)
            diff(g - 1)
        sums(3, 0)
        weave_m(2, 1)
        quant_m(2, 0)
        weave_y(1)
        quant_m(2, 1)
        turn_y(1)
        weave_m(3, 0)
        quant_y(1)
        store_scales(False)
        quant_m(3, 0)
        sums(3, 1, "SSSV")
        diff(2)
        weave_m(3, 1, 0)
        weave_m(3, 1, 1)
        quant_m(3, 1, 0)
        quant_m(3, 1, 1)
        for j in range(4):
            diff_pass(3, j, 0)
        for i in range(4):
            turn_y_pe(2, i)
        for j in range(4):
            diff_pass(3, j, 1)
        weave_y(2)
        turn_y_out(2, 0, "S")
        turn_y_out(2, 1, "S")
        turn_y_out(2, 2, "V")
        quant_y(2)
        turn_y_out(2, 3, "V")
        for part in range(2):
            for j in range(4):
                diff_out(3, j, part)
        turn_y_pe(3, 0)
        turn_y_pe(3, 1)
        weave_y(3, 0)
        turn_y_out(3, 0, "S")
        turn_y_pe(3, 2)
        turn_y_pe(3, 3)
        weave_y(3, 1)
        turn_y_out(3, 1, "S")
        quant_y(3, 0)
        quant_y(3, 1)
        turn_y_out(3, 2, "S")
        turn_y_out(3, 3, "S")
        store_scales(True)
